import numpy as np
import ml_dtypes


def mxq(x, axis, fmt="e4m3"):
    dtype, down = {"e4m3": (ml_dtypes.float8_e4m3fn, 7), "e5m2": (ml_dtypes.float8_e5m2, 14)}[fmt]
    v = np.moveaxis(np.asarray(x, np.float32).astype(ml_dtypes.bfloat16).astype(np.float64), axis, -1)
    blocks = v.reshape(v.shape[:-1] + (-1, 32))
    amax = np.abs(blocks).max(-1, keepdims=True)
    byte = np.maximum(np.where(amax > 0, np.frexp(amax)[1] - 1 + 127, 0) - down, 1)
    scale = np.exp2(byte - 127.0)
    codes = (blocks / scale).astype(np.float32).astype(dtype).astype(np.float64)
    return np.moveaxis((codes * scale).reshape(v.shape), -1, axis)


WIDE = False


def mx_kscale(k):
    if not WIDE:
        return np.ones(k)
    levels = np.array([10, -10, 5, -5, 0])
    if k % 512:
        return np.exp2(np.random.permutation(np.resize(levels, k // 32))).repeat(32)
    a = np.empty((k // 512, 16))
    for p in range(k // 512):
        a[p, :8] = np.random.permutation(np.resize(levels, 8))
        for g in range(8):
            far = levels[np.abs(levels - a[p, g]) >= 10]
            a[p, g + 8] = far[np.random.randint(len(far))]
    return np.exp2(a.ravel()).repeat(32)


def f64(x):
    return np.asarray(x).astype(np.float64)


def striped8(idx):
    return np.asarray(idx).reshape(8, -1, 16).transpose(0, 2, 1).reshape(128, -1).astype(np.uint16)


def unstriped8(offs):
    return offs.reshape(8, 16, -1).transpose(0, 2, 1).reshape(8, -1).astype(np.int64)


def pick8(x, idx, run):
    r = np.arange(len(x))
    return x[r[:, None], idx[r % (8 * run) // run]]


E2M1 = np.array([0.0, 0.5, 1.0, 1.5, 2.0, 3.0, 4.0, 6.0, -0.0, -0.5, -1.0, -1.5, -2.0, -3.0, -4.0, -6.0])


def pack_weight(w, fmt):
    k, n = w.shape
    w = f64(np.asarray(w, np.float32).astype(ml_dtypes.bfloat16)).reshape(k // 32, 32, n)
    amax = np.abs(w).max(1)
    if fmt == "e4m3":
        byte = np.frexp(amax)[1] - 1 + 127 - 7
    else:
        mant, ex = np.frexp(amax / 6.0)
        byte = np.where(mant > 0.5, ex, ex - 1) + 127
    byte = np.clip(np.where(amax > 0, byte, 1), 1, 254)
    scaled = (w * np.exp2(127.0 - byte)[:, None, :]).reshape(k, n).astype(np.float32)
    by_word = np.ascontiguousarray(scaled.reshape(k // 512, 128, 4, n).transpose(0, 1, 3, 2))
    if fmt == "e4m3":
        words = by_word.astype(ml_dtypes.float8_e4m3fn).view(np.uint8)
    else:
        c = by_word.astype(ml_dtypes.float4_e2m1fn).view(np.uint8) & 0xF
        words = (c[..., 0::2] | (c[..., 1::2] << 4)).reshape(k // 512, 128, 2 * n)
    return np.ascontiguousarray(words), np.ascontiguousarray(byte.astype(np.uint8).reshape(k // 512, 16, n))


def unpack_weight(words, scales, fmt):
    g, _, n = scales.shape
    words = np.ascontiguousarray(words).reshape(g, 128, n, -1)
    if fmt == "e4m3":
        vals = words.view(ml_dtypes.float8_e4m3fn).astype(np.float64)
    else:
        nib = np.empty((g, 128, n, 4), np.uint8)
        nib[..., 0::2] = words & 0xF
        nib[..., 1::2] = words >> 4
        vals = E2M1[nib]
    vals = vals * np.repeat(np.exp2(scales.astype(np.float64) - 127.0), 8, axis=1)[..., None]
    return vals.transpose(0, 1, 3, 2).reshape(g * 512, n)


D, T, U, X, I, Q = 512, 1024, 1024, 1024, 512, 128


def setup_inputs():
    n = np.random.standard_normal
    idx = np.stack([np.random.permutation(T)[:I] for _ in range(8)])
    idx2 = np.stack([np.random.permutation(U)[:I] for _ in range(8)])
    idx3 = np.stack([np.random.permutation(X)[:I] for _ in range(8)])
    idx4 = np.stack([np.random.permutation(X)[:I] for _ in range(8)])
    fd = mx_kscale(D)
    keysp = pack_weight(n((D, T)) / fd[:, None], "e4m3")
    notesp = pack_weight(n((D, U)) / fd[:, None], "e2m1")
    usersp = pack_weight(n((D, X)) / fd[:, None], "e4m3")
    return {
        "query": (n((D, Q)) * 1.0 / np.sqrt(D) * fd[:, None]).astype(np.float32),
        "keys_words": keysp[0],
        "keys_scales": keysp[1],
        "notes_words": notesp[0],
        "notes_scales": notesp[1],
        "users_words": usersp[0],
        "users_scales": usersp[1],
        "offs": striped8(idx),
        "offs2": striped8(idx2),
        "offs3": striped8(idx3),
        "offs4": striped8(idx4),
    }


def reference(query, keys_words, keys_scales, notes_words, notes_scales, users_words, users_scales, offs, offs2, offs3, offs4):
    idx = unstriped8(offs)
    idx2 = unstriped8(offs2)
    idx3 = unstriped8(offs3)
    idx4 = unstriped8(offs4)
    keysu = unpack_weight(keys_words, keys_scales, "e4m3")
    notesu = unpack_weight(notes_words, notes_scales, "e2m1")
    usersu = unpack_weight(users_words, users_scales, "e4m3")
    queryq = mxq(f64(query), 0, "e4m3")
    a = queryq.T @ keysu
    b = queryq.T @ notesu
    c0 = queryq.T @ usersu
    w = pick8(a, idx, 16) - pick8(b, idx2, 16)
    w1 = np.pad(w, ((0, 0), (1, 0)))[:, :I]
    v = np.maximum(w, w1)
    f1 = np.zeros((Q, X))
    f1[np.arange(Q)[:, None], idx3[np.arange(Q) % 128 // 16]] = v
    cc = c0 + f1
    y = pick8(cc, idx4, 16) - w1
    return y

@@ -1,0 +1,135 @@
+from contextlib import ExitStack
+
+import concourse.mybir as mybir
+
+D, T, I, Q = 512, 1024, 512, 128
+FLOPS = 3 * 2 * D * Q * T
+
+F32 = mybir.dt.float32
+BF16 = mybir.dt.bfloat16
+I32 = mybir.dt.int32
+U32 = mybir.dt.uint32
+U16 = mybir.dt.uint16
+U8 = mybir.dt.uint8
+FP8X4 = mybir.dt.float8_e4m3fn_x4
+FP4X4 = mybir.dt.float4_e2m1fn_x4
+ALU = mybir.AluOpType
+COPY = mybir.ActivationFunctionType.Copy
+
+P = 128
+PACK = 4
+CHUNK = 256
+BANK = 512
+HALF = I // 2
+LEAD = 4
+
+
+def tile_attend_strides_three_kernel(tc, query, keys_words, keys_scales, notes_words, notes_scales,
+                                      users_words, users_scales, offs, offs2, offs3, offs4, out):
+    nc = tc.nc
+    with ExitStack() as ctx:
+        sb = ctx.enter_context(tc.tile_pool(name="sb", bufs=1))
+        ps = ctx.enter_context(tc.psum_pool(name="ps", bufs=1))
+
+        raw = sb.tile([P, PACK, Q], F32, name="raw")
+        grouped = sb.tile([P, Q, PACK], BF16, name="grouped", align_bytes=64)
+        q_codes = sb.tile([P, Q], U32, name="q_codes", align_bytes=64)
+        q_plane = sb.tile([P, Q], U8, name="q_plane", align_bytes=64)
+        keys_w = sb.tile([P, T], U32, name="keys_w", align_bytes=64)
+        notes_w = sb.tile([P, 2 * T], U8, name="notes_w", align_bytes=64)
+        users_w = sb.tile([P, T], U32, name="users_w", align_bytes=64)
+        keys_s = sb.tile([P, T], U8, name="keys_s", align_bytes=64)
+        notes_s = sb.tile([P, T], U8, name="notes_s", align_bytes=64)
+        users_s = sb.tile([P, T], U8, name="users_s", align_bytes=64)
+        l1 = sb.tile([P, I // 16], U16, name="l1")
+        l2 = sb.tile([P, I // 16], U16, name="l2")
+        l3 = sb.tile([P, I // 16], U16, name="l3")
+        l4 = sb.tile([P, I // 16], U16, name="l4")
+        a_sb = sb.tile([P, T], F32, name="a_sb")
+        b_sb = sb.tile([P, T], F32, name="b_sb")
+        f1 = sb.tile([P, T], F32, name="f1")
+        cc = sb.tile([P, T], F32, name="cc")
+        b_got = [sb.tile([P, HALF], F32, name="b_got%d" % h) for h in range(2)]
+        w_pad = sb.tile([P, LEAD + I], F32, name="w_pad")
+        v = sb.tile([P, I], F32, name="v")
+        res = [sb.tile([P, HALF], F32, name="res%d" % h) for h in range(2)]
+
+        def load_scales(plane, scales, quad):
+            nc.sync.dma_start(out=plane[32 * quad:32 * quad + 4, :].bitcast(I32),
+                              in_=scales[0, 4 * quad:4 * quad + 4, :].bitcast(I32))
+
+        def half_list(lst, h):
+            return lst[:, h * (HALF // 16):(h + 1) * (HALF // 16)]
+
+        nc.vector.memset(notes_s[:].bitcast(U32), 0)
+        nc.vector.memset(keys_s[:].bitcast(U32), 0)
+        nc.vector.memset(users_s[:].bitcast(U32), 0)
+        nc.vector.memset(f1[:], 0.0)
+        nc.vector.memset(w_pad[:, LEAD - 1:LEAD], 0.0)
+
+        nc.sync.dma_start(out=raw[:], in_=query.rearrange("(p j) q -> p j q", j=PACK))
+        load_scales(notes_s, notes_scales, 0)
+        load_scales(notes_s, notes_scales, 1)
+        nc.sync.dma_start(out=notes_w[:].bitcast(I32), in_=notes_words[0].bitcast(I32))
+        load_scales(notes_s, notes_scales, 2)
+        load_scales(notes_s, notes_scales, 3)
+        nc.sync.dma_start(out=keys_w[:].bitcast(I32),
+                          in_=keys_words[0].rearrange("p n t -> p (n t)").bitcast(I32))
+        for quad in range(4):
+            load_scales(keys_s, keys_scales, quad)
+        nc.sync.dma_start(l2[:], offs2)
+        nc.sync.dma_start(l1[:], offs)
+        nc.sync.dma_start(l3[:], offs3)
+        nc.sync.dma_start(out=users_w[:].bitcast(I32),
+                          in_=users_words[0].rearrange("p n t -> p (n t)").bitcast(I32))
+        for quad in range(4):
+            load_scales(users_s, users_scales, quad)
+        nc.sync.dma_start(l4[:], offs4)
+
+        nc.vector.tensor_copy(out=grouped[:], in_=raw[:].rearrange("p j q -> p q j"))
+        nc.vector.quantize_mx(out=q_codes[:].bitcast(FP8X4), scales=q_plane[:],
+                              in_=grouped[:].rearrange("p q j -> p (q j)"))
+
+        def scores(acc, words, plane):
+            nc.tensor.matmul_mx(out=acc, lhsT=q_codes[:].bitcast(FP8X4), lhsT_scale=q_plane[:],
+                                rhs=words, rhs_scale=plane, start=True, stop=True)
+
+        for c in range(T // CHUNK):
+            cols = slice(c * CHUNK, (c + 1) * CHUNK)
+            acc = ps.tile([P, CHUNK], F32, name="b_ps", tag="bank%d" % c)
+            scores(acc[:], notes_w[:, 2 * cols.start:2 * cols.stop].bitcast(FP4X4), notes_s[:, cols])
+            nc.scalar.activation(b_sb[:, cols], acc[:], COPY)
+        for c in range(T // CHUNK):
+            cols = slice(c * CHUNK, (c + 1) * CHUNK)
+            acc = ps.tile([P, CHUNK], F32, name="a_ps", tag="bank%d" % (4 + c))
+            scores(acc[:], keys_w[:, cols].bitcast(FP8X4), keys_s[:, cols])
+            nc.vector.tensor_copy(out=a_sb[:, cols], in_=acc[:])
+        c_ps = []
+        for c in range(T // BANK):
+            cols = slice(c * BANK, (c + 1) * BANK)
+            acc = ps.tile([P, BANK], F32, name="c_ps", tag="bank%d" % c)
+            scores(acc[:], users_w[:, cols].bitcast(FP8X4), users_s[:, cols])
+            c_ps.append(acc)
+
+        a_got = sb.tile([P, HALF], F32, name="a_got")
+        c_got = sb.tile([P, HALF], F32, name="c_got")
+        w_half = [w_pad[:, LEAD + h * HALF:LEAD + (h + 1) * HALF] for h in range(2)]
+        w1_half = [w_pad[:, LEAD - 1 + h * HALF:LEAD - 1 + (h + 1) * HALF] for h in range(2)]
+        v_half = [v[:, h * HALF:(h + 1) * HALF] for h in range(2)]
+        for h in range(2):
+            nc.scalar.activation(b_got[h][:], b_sb[:].indirect(half_list(l2, h)), COPY)
+        nc.vector.tensor_tensor(w_half[0], a_sb[:].indirect(half_list(l1, 0)), b_got[0][:], ALU.subtract)
+        nc.scalar.activation(a_got[:], a_sb[:].indirect(half_list(l1, 1)), COPY)
+        nc.vector.tensor_tensor(v_half[0], w_half[0], w1_half[0], ALU.max)
+        nc.vector.tensor_tensor(w_half[1], a_got[:], b_got[1][:], ALU.subtract)
+        nc.vector.tensor_copy(f1[:].indirect(half_list(l3, 0)), v_half[0])
+        nc.vector.tensor_tensor(v_half[1], w_half[1], w1_half[1], ALU.max)
+        nc.vector.tensor_copy(f1[:].indirect(half_list(l3, 1)), v_half[1])
+        for c in range(T // BANK):
+            cols = slice(c * BANK, (c + 1) * BANK)
+            nc.vector.tensor_tensor(cc[:, cols], c_ps[c][:], f1[:, cols], ALU.add)
+        nc.vector.tensor_tensor(res[0][:], cc[:].indirect(half_list(l4, 0)), w1_half[0], ALU.subtract)
+        nc.sync.dma_start(out=out[:, 0:HALF], in_=res[0][:])
+        nc.scalar.activation(c_got[:], cc[:].indirect(half_list(l4, 1)), COPY)
+        nc.vector.tensor_tensor(res[1][:], c_got[:], w1_half[1], ALU.subtract)
+        nc.sync.dma_start(out=out[:, HALF:I], in_=res[1][:])

@@ -32,7 +32,7 @@ def tile_attend_strides_three_kernel(tc, query, keys_words, keys_scales, notes_w
         ps = ctx.enter_context(tc.psum_pool(name="ps", bufs=1))
 
         raw = sb.tile([P, PACK, Q], F32, name="raw")
-        grouped = sb.tile([P, Q, PACK], BF16, name="grouped", align_bytes=64)
+        grouped = [sb.tile([P, Q // 2, PACK], BF16, name="grouped%d" % h, align_bytes=64) for h in range(2)]
         q_codes = sb.tile([P, Q], U32, name="q_codes", align_bytes=64)
         q_plane = sb.tile([P, Q], U8, name="q_plane", align_bytes=64)
         keys_w = sb.tile([P, T], U32, name="keys_w", align_bytes=64)
@@ -86,9 +86,12 @@ def tile_attend_strides_three_kernel(tc, query, keys_words, keys_scales, notes_w
             load_scales(users_s, users_scales, quad)
         nc.sync.dma_start(l4[:], offs4)
 
-        nc.vector.tensor_copy(out=grouped[:], in_=raw[:].rearrange("p j q -> p q j"))
-        nc.vector.quantize_mx(out=q_codes[:].bitcast(FP8X4), scales=q_plane[:],
-                              in_=grouped[:].rearrange("p q j -> p (q j)"))
+        q_halves = [slice(h * Q // 2, (h + 1) * Q // 2) for h in range(2)]
+        for h, rows in enumerate(q_halves):
+            nc.vector.tensor_copy(out=grouped[h][:], in_=raw[:, :, rows].rearrange("p j q -> p q j"))
+        for h, rows in enumerate(q_halves):
+            nc.vector.quantize_mx(out=q_codes[:, rows].bitcast(FP8X4), scales=q_plane[:, rows],
+                                  in_=grouped[h][:].rearrange("p q j -> p (q j)"))
 
         def scores(acc, words, plane):
             nc.tensor.matmul_mx(out=acc, lhsT=q_codes[:].bitcast(FP8X4), lhsT_scale=q_plane[:],
@@ -125,9 +128,12 @@ def tile_attend_strides_three_kernel(tc, query, keys_words, keys_scales, notes_w
         nc.vector.tensor_copy(f1[:].indirect(half_list(l3, 0)), v_half[0])
         nc.vector.tensor_tensor(v_half[1], w_half[1], w1_half[1], ALU.max)
         nc.vector.tensor_copy(f1[:].indirect(half_list(l3, 1)), v_half[1])
-        for c in range(T // BANK):
-            cols = slice(c * BANK, (c + 1) * BANK)
-            nc.vector.tensor_tensor(cc[:, cols], c_ps[c][:], f1[:, cols], ALU.add)
+        split = T - 256
+        c_sb = sb.tile([P, T - split], F32, name="c_sb")
+        nc.scalar.copy(c_sb[:], c_ps[1][:, split - BANK:BANK])
+        nc.gpsimd.tensor_tensor(cc[:, split:T], c_sb[:], f1[:, split:T], ALU.add)
+        nc.vector.tensor_tensor(cc[:, 0:BANK], c_ps[0][:], f1[:, 0:BANK], ALU.add)
+        nc.vector.tensor_tensor(cc[:, BANK:split], c_ps[1][:, 0:split - BANK], f1[:, BANK:split], ALU.add)
         nc.vector.tensor_tensor(res[0][:], cc[:].indirect(half_list(l4, 0)), w1_half[0], ALU.subtract)
         nc.sync.dma_start(out=out[:, 0:HALF], in_=res[0][:])
         nc.scalar.activation(c_got[:], cc[:].indirect(half_list(l4, 1)), COPY)

@@ -38,9 +38,9 @@ def tile_attend_strides_three_kernel(tc, query, keys_words, keys_scales, notes_w
         keys_w = sb.tile([P, T], U32, name="keys_w", align_bytes=64)
         notes_w = sb.tile([P, 2 * T], U8, name="notes_w", align_bytes=64)
         users_w = sb.tile([P, T], U32, name="users_w", align_bytes=64)
-        keys_s = sb.tile([P, T], U8, name="keys_s", align_bytes=64)
+        keys_s = sb.tile([P, CHUNK], U8, name="keys_s", align_bytes=64)
         notes_s = sb.tile([P, T], U8, name="notes_s", align_bytes=64)
-        users_s = sb.tile([P, T], U8, name="users_s", align_bytes=64)
+        users_s = sb.tile([P, CHUNK], U8, name="users_s", align_bytes=64)
         l1 = sb.tile([P, I // 16], U16, name="l1")
         l2 = sb.tile([P, I // 16], U16, name="l2")
         l3 = sb.tile([P, I // 16], U16, name="l3")
@@ -55,8 +55,12 @@ def tile_attend_strides_three_kernel(tc, query, keys_words, keys_scales, notes_w
         res = [sb.tile([P, HALF], F32, name="res%d" % h) for h in range(2)]
 
         def load_scales(plane, scales, quad):
-            nc.sync.dma_start(out=plane[32 * quad:32 * quad + 4, :].bitcast(I32),
-                              in_=scales[0, 4 * quad:4 * quad + 4, :].bitcast(I32))
+            nc.sync.dma_start(out=plane[quad:P:32, :].bitcast(I32),
+                              in_=scales[0, quad:16:4, :].bitcast(I32))
+
+        def load_packed(planes, scales, quad):
+            nc.sync.dma_start(out=planes[32 * quad:32 * quad + 16, :].bitcast(I32),
+                              in_=scales[0, 4 * quad:4 * quad + 4, :].bitcast(I32).rearrange("j (c n) -> c j n", c=4))
 
         def half_list(lst, h):
             return lst[:, h * (HALF // 16):(h + 1) * (HALF // 16)]
@@ -76,14 +80,14 @@ def tile_attend_strides_three_kernel(tc, query, keys_words, keys_scales, notes_w
         nc.sync.dma_start(out=keys_w[:].bitcast(I32),
                           in_=keys_words[0].rearrange("p n t -> p (n t)").bitcast(I32))
         for quad in range(4):
-            load_scales(keys_s, keys_scales, quad)
+            load_packed(keys_s, keys_scales, quad)
         nc.sync.dma_start(l2[:], offs2)
         nc.sync.dma_start(l1[:], offs)
         nc.sync.dma_start(l3[:], offs3)
         nc.sync.dma_start(out=users_w[:].bitcast(I32),
                           in_=users_words[0].rearrange("p n t -> p (n t)").bitcast(I32))
         for quad in range(4):
-            load_scales(users_s, users_scales, quad)
+            load_packed(users_s, users_scales, quad)
         nc.sync.dma_start(l4[:], offs4)
 
         q_halves = [slice(h * Q // 2, (h + 1) * Q // 2) for h in range(2)]
@@ -105,13 +109,15 @@ def tile_attend_strides_three_kernel(tc, query, keys_words, keys_scales, notes_w
         for c in range(T // CHUNK):
             cols = slice(c * CHUNK, (c + 1) * CHUNK)
             acc = ps.tile([P, CHUNK], F32, name="a_ps", tag="bank%d" % (4 + c))
-            scores(acc[:], keys_w[:, cols].bitcast(FP8X4), keys_s[:, cols])
+            scores(acc[:], keys_w[:, cols].bitcast(FP8X4), keys_s[4 * c:P, :])
             nc.vector.tensor_copy(out=a_sb[:, cols], in_=acc[:])
         c_ps = []
         for c in range(T // BANK):
-            cols = slice(c * BANK, (c + 1) * BANK)
             acc = ps.tile([P, BANK], F32, name="c_ps", tag="bank%d" % c)
-            scores(acc[:], users_w[:, cols].bitcast(FP8X4), users_s[:, cols])
+            for k in range(2):
+                n = 2 * c + k
+                scores(acc[:, k * CHUNK:(k + 1) * CHUNK],
+                       users_w[:, n * CHUNK:(n + 1) * CHUNK].bitcast(FP8X4), users_s[4 * n:P, :])
             c_ps.append(acc)
 
         a_got = sb.tile([P, HALF], F32, name="a_got")

from contextlib import ExitStack

import concourse.mybir as mybir

D, T, I, Q = 512, 1024, 512, 128
FLOPS = 3 * 2 * D * Q * T

F32 = mybir.dt.float32
BF16 = mybir.dt.bfloat16
I32 = mybir.dt.int32
U32 = mybir.dt.uint32
U16 = mybir.dt.uint16
U8 = mybir.dt.uint8
FP8X4 = mybir.dt.float8_e4m3fn_x4
FP4X4 = mybir.dt.float4_e2m1fn_x4
ALU = mybir.AluOpType
COPY = mybir.ActivationFunctionType.Copy

P = 128
PACK = 4
CHUNK = 256
BANK = 512
HALF = I // 2
LEAD = 4


def tile_attend_strides_three_kernel(tc, query, keys_words, keys_scales, notes_words, notes_scales,
                                      users_words, users_scales, offs, offs2, offs3, offs4, out):
    nc = tc.nc
    with ExitStack() as ctx:
        sb = ctx.enter_context(tc.tile_pool(name="sb", bufs=1))
        ps = ctx.enter_context(tc.psum_pool(name="ps", bufs=1))

        raw = sb.tile([P, PACK, Q], F32, name="raw")
        grouped = [sb.tile([P, Q // 2, PACK], BF16, name="grouped%d" % h, align_bytes=64) for h in range(2)]
        q_codes = sb.tile([P, Q], U32, name="q_codes", align_bytes=64)
        q_plane = sb.tile([P, Q], U8, name="q_plane", align_bytes=64)
        keys_w = sb.tile([P, T], U32, name="keys_w", align_bytes=64)
        notes_w = sb.tile([P, 2 * T], U8, name="notes_w", align_bytes=64)
        users_w = sb.tile([P, T], U32, name="users_w", align_bytes=64)
        keys_s = sb.tile([P, CHUNK], U8, name="keys_s", align_bytes=64)
        notes_s = sb.tile([P, T], U8, name="notes_s", align_bytes=64)
        users_s = sb.tile([P, CHUNK], U8, name="users_s", align_bytes=64)
        l1 = sb.tile([P, I // 16], U16, name="l1")
        l2 = sb.tile([P, I // 16], U16, name="l2")
        l3 = sb.tile([P, I // 16], U16, name="l3")
        l4 = sb.tile([P, I // 16], U16, name="l4")
        a_sb = sb.tile([P, T], F32, name="a_sb")
        b_sb = sb.tile([P, T], F32, name="b_sb")
        f1 = sb.tile([P, T], F32, name="f1")
        cc = sb.tile([P, T], F32, name="cc")
        b_got = [sb.tile([P, HALF], F32, name="b_got%d" % h) for h in range(2)]
        w_pad = sb.tile([P, LEAD + I], F32, name="w_pad")
        v = sb.tile([P, I], F32, name="v")
        res = [sb.tile([P, HALF], F32, name="res%d" % h) for h in range(2)]

        def load_scales(plane, scales, quad):
            nc.sync.dma_start(out=plane[quad:P:32, :].bitcast(I32),
                              in_=scales[0, quad:16:4, :].bitcast(I32))

        def load_packed(planes, scales, quad):
            nc.sync.dma_start(out=planes[32 * quad:32 * quad + 16, :].bitcast(I32),
                              in_=scales[0, 4 * quad:4 * quad + 4, :].bitcast(I32).rearrange("j (c n) -> c j n", c=4))

        def half_list(lst, h):
            return lst[:, h * (HALF // 16):(h + 1) * (HALF // 16)]

        nc.vector.memset(notes_s[:].bitcast(U32), 0)
        nc.vector.memset(keys_s[:].bitcast(U32), 0)
        nc.vector.memset(users_s[:].bitcast(U32), 0)
        nc.vector.memset(f1[:], 0.0)
        nc.vector.memset(w_pad[:, LEAD - 1:LEAD], 0.0)

        nc.sync.dma_start(out=raw[:], in_=query.rearrange("(p j) q -> p j q", j=PACK))
        load_scales(notes_s, notes_scales, 0)
        load_scales(notes_s, notes_scales, 1)
        nc.sync.dma_start(out=notes_w[:].bitcast(I32), in_=notes_words[0].bitcast(I32))
        load_scales(notes_s, notes_scales, 2)
        load_scales(notes_s, notes_scales, 3)
        nc.sync.dma_start(out=keys_w[:].bitcast(I32),
                          in_=keys_words[0].rearrange("p n t -> p (n t)").bitcast(I32))
        for quad in range(4):
            load_packed(keys_s, keys_scales, quad)
        nc.sync.dma_start(l2[:], offs2)
        nc.sync.dma_start(l1[:], offs)
        nc.sync.dma_start(l3[:], offs3)
        nc.sync.dma_start(out=users_w[:].bitcast(I32),
                          in_=users_words[0].rearrange("p n t -> p (n t)").bitcast(I32))
        for quad in range(4):
            load_packed(users_s, users_scales, quad)
        nc.sync.dma_start(l4[:], offs4)

        q_halves = [slice(h * Q // 2, (h + 1) * Q // 2) for h in range(2)]
        for h, rows in enumerate(q_halves):
            nc.vector.tensor_copy(out=grouped[h][:], in_=raw[:, :, rows].rearrange("p j q -> p q j"))
        for h, rows in enumerate(q_halves):
            nc.vector.quantize_mx(out=q_codes[:, rows].bitcast(FP8X4), scales=q_plane[:, rows],
                                  in_=grouped[h][:].rearrange("p q j -> p (q j)"))

        def scores(acc, words, plane):
            nc.tensor.matmul_mx(out=acc, lhsT=q_codes[:].bitcast(FP8X4), lhsT_scale=q_plane[:],
                                rhs=words, rhs_scale=plane, start=True, stop=True)

        for c in range(T // CHUNK):
            cols = slice(c * CHUNK, (c + 1) * CHUNK)
            acc = ps.tile([P, CHUNK], F32, name="b_ps", tag="bank%d" % c)
            scores(acc[:], notes_w[:, 2 * cols.start:2 * cols.stop].bitcast(FP4X4), notes_s[:, cols])
            nc.scalar.activation(b_sb[:, cols], acc[:], COPY)
        for c in range(T // CHUNK):
            cols = slice(c * CHUNK, (c + 1) * CHUNK)
            acc = ps.tile([P, CHUNK], F32, name="a_ps", tag="bank%d" % (4 + c))
            scores(acc[:], keys_w[:, cols].bitcast(FP8X4), keys_s[4 * c:P, :])
            nc.vector.tensor_copy(out=a_sb[:, cols], in_=acc[:])
        c_ps = []
        for c in range(T // BANK):
            acc = ps.tile([P, BANK], F32, name="c_ps", tag="bank%d" % c)
            for k in range(2):
                n = 2 * c + k
                scores(acc[:, k * CHUNK:(k + 1) * CHUNK],
                       users_w[:, n * CHUNK:(n + 1) * CHUNK].bitcast(FP8X4), users_s[4 * n:P, :])
            c_ps.append(acc)

        a_got = sb.tile([P, HALF], F32, name="a_got")
        c_got = sb.tile([P, HALF], F32, name="c_got")
        w_half = [w_pad[:, LEAD + h * HALF:LEAD + (h + 1) * HALF] for h in range(2)]
        w1_half = [w_pad[:, LEAD - 1 + h * HALF:LEAD - 1 + (h + 1) * HALF] for h in range(2)]
        v_half = [v[:, h * HALF:(h + 1) * HALF] for h in range(2)]
        for h in range(2):
            nc.scalar.activation(b_got[h][:], b_sb[:].indirect(half_list(l2, h)), COPY)
        nc.vector.tensor_tensor(w_half[0], a_sb[:].indirect(half_list(l1, 0)), b_got[0][:], ALU.subtract)
        nc.scalar.activation(a_got[:], a_sb[:].indirect(half_list(l1, 1)), COPY)
        nc.vector.tensor_tensor(v_half[0], w_half[0], w1_half[0], ALU.max)
        nc.vector.tensor_tensor(w_half[1], a_got[:], b_got[1][:], ALU.subtract)
        nc.vector.tensor_copy(f1[:].indirect(half_list(l3, 0)), v_half[0])
        nc.vector.tensor_tensor(v_half[1], w_half[1], w1_half[1], ALU.max)
        nc.vector.tensor_copy(f1[:].indirect(half_list(l3, 1)), v_half[1])
        split = T - 256
        c_sb = sb.tile([P, T - split], F32, name="c_sb")
        nc.scalar.copy(c_sb[:], c_ps[1][:, split - BANK:BANK])
        nc.gpsimd.tensor_tensor(cc[:, split:T], c_sb[:], f1[:, split:T], ALU.add)
        nc.vector.tensor_tensor(cc[:, 0:BANK], c_ps[0][:], f1[:, 0:BANK], ALU.add)
        nc.vector.tensor_tensor(cc[:, BANK:split], c_ps[1][:, 0:split - BANK], f1[:, BANK:split], ALU.add)
        nc.vector.tensor_tensor(res[0][:], cc[:].indirect(half_list(l4, 0)), w1_half[0], ALU.subtract)
        nc.sync.dma_start(out=out[:, 0:HALF], in_=res[0][:])
        nc.scalar.activation(c_got[:], cc[:].indirect(half_list(l4, 1)), COPY)
        nc.vector.tensor_tensor(res[1][:], c_got[:], w1_half[1], ALU.subtract)
        nc.sync.dma_start(out=out[:, HALF:I], in_=res[1][:])
